import numpy as np
import ml_dtypes


def mxq(x, axis, fmt="e4m3"):
    dtype, down = {"e4m3": (ml_dtypes.float8_e4m3fn, 7), "e5m2": (ml_dtypes.float8_e5m2, 14)}[fmt]
    v = np.moveaxis(np.asarray(x, np.float32).astype(ml_dtypes.bfloat16).astype(np.float64), axis, -1)
    blocks = v.reshape(v.shape[:-1] + (-1, 32))
    amax = np.abs(blocks).max(-1, keepdims=True)
    byte = np.maximum(np.where(amax > 0, np.frexp(amax)[1] - 1 + 127, 0) - down, 1)
    scale = np.exp2(byte - 127.0)
    codes = (blocks / scale).astype(np.float32).astype(dtype).astype(np.float64)
    return np.moveaxis((codes * scale).reshape(v.shape), -1, axis)


WIDE = False


def mx_kscale(k):
    if not WIDE:
        return np.ones(k)
    levels = np.array([10, -10, 5, -5, 0])
    if k % 512:
        return np.exp2(np.random.permutation(np.resize(levels, k // 32))).repeat(32)
    a = np.empty((k // 512, 16))
    for p in range(k // 512):
        a[p, :8] = np.random.permutation(np.resize(levels, 8))
        for g in range(8):
            far = levels[np.abs(levels - a[p, g]) >= 10]
            a[p, g + 8] = far[np.random.randint(len(far))]
    return np.exp2(a.ravel()).repeat(32)


def f64(x):
    return np.asarray(x).astype(np.float64)


def striped(idx):
    return np.tile(idx.reshape(-1, 16).T, (8, 1)).astype(np.uint16)


def unstriped(offs):
    return offs[:16].T.reshape(-1).astype(np.int64)


E2M1 = np.array([0.0, 0.5, 1.0, 1.5, 2.0, 3.0, 4.0, 6.0, -0.0, -0.5, -1.0, -1.5, -2.0, -3.0, -4.0, -6.0])


def pack_weight(w, fmt):
    k, n = w.shape
    w = f64(np.asarray(w, np.float32).astype(ml_dtypes.bfloat16)).reshape(k // 32, 32, n)
    amax = np.abs(w).max(1)
    if fmt == "e4m3":
        byte = np.frexp(amax)[1] - 1 + 127 - 7
    else:
        mant, ex = np.frexp(amax / 6.0)
        byte = np.where(mant > 0.5, ex, ex - 1) + 127
    byte = np.clip(np.where(amax > 0, byte, 1), 1, 254)
    scaled = (w * np.exp2(127.0 - byte)[:, None, :]).reshape(k, n).astype(np.float32)
    by_word = np.ascontiguousarray(scaled.reshape(k // 512, 128, 4, n).transpose(0, 1, 3, 2))
    if fmt == "e4m3":
        words = by_word.astype(ml_dtypes.float8_e4m3fn).view(np.uint8)
    else:
        c = by_word.astype(ml_dtypes.float4_e2m1fn).view(np.uint8) & 0xF
        words = (c[..., 0::2] | (c[..., 1::2] << 4)).reshape(k // 512, 128, 2 * n)
    return np.ascontiguousarray(words), np.ascontiguousarray(byte.astype(np.uint8).reshape(k // 512, 16, n))


def unpack_weight(words, scales, fmt):
    g, _, n = scales.shape
    words = np.ascontiguousarray(words).reshape(g, 128, n, -1)
    if fmt == "e4m3":
        vals = words.view(ml_dtypes.float8_e4m3fn).astype(np.float64)
    else:
        nib = np.empty((g, 128, n, 4), np.uint8)
        nib[..., 0::2] = words & 0xF
        nib[..., 1::2] = words >> 4
        vals = E2M1[nib]
    vals = vals * np.repeat(np.exp2(scales.astype(np.float64) - 127.0), 8, axis=1)[..., None]
    return vals.transpose(0, 1, 3, 2).reshape(g * 512, n)


def gelu(v):
    return 0.5 * v * (1.0 + np.tanh(np.sqrt(2.0 / np.pi) * (v + 0.044715 * v**3)))


K, T, S, S2 = 1024, 2048, 1024, 512


def setup_inputs():
    n = np.random.standard_normal
    s = mx_kscale(K)[:, None]
    d = {}
    d["tab_words"], d["tab_scales"] = pack_weight(n((K, T)) * s, "e4m3")
    d["offs"] = striped(np.random.permutation(T)[:S])
    d["offs2"] = striped(np.random.permutation(T)[:S2])
    d["w"] = (n((K, K)) / s / s.T / K).astype(np.float32)
    d["ws_words"], d["ws_scales"] = pack_weight(n((K, S2)) / s / K**0.5, "e2m1")
    d["wf_words"], d["wf_scales"] = pack_weight(1.2 * n((K, S)) / s / K**0.5, "e4m3")
    d["gain"] = np.exp(0.4 * n(S2)).astype(np.float32)
    return d


def reference(tab_words, tab_scales, offs, offs2, w, ws_words, ws_scales, wf_words, wf_scales, gain):
    TW = unpack_weight(tab_words, tab_scales, "e4m3")
    v = TW[:, unstriped(offs)]
    v2 = TW[:, unstriped(offs2)]
    ws = unpack_weight(ws_words, ws_scales, "e2m1")
    wf = unpack_weight(wf_words, wf_scales, "e4m3")
    h = np.abs(mxq(f64(w), 0, "e4m3").T @ v)
    hq = mxq(h, 0, "e4m3")
    e = v2.T @ hq + ws.T @ v
    f = v2.T @ wf
    return f64(gain)[:, None] * np.maximum(e, f)

@@ -1,0 +1,260 @@
+from contextlib import ExitStack
+
+import concourse.mybir as mybir
+
+K, T, S, S2 = 1024, 2048, 1024, 512
+FLOPS = 2 * K * K * S + 3 * 2 * K * S2 * S
+
+F32 = mybir.dt.float32
+BF16 = mybir.dt.bfloat16
+I32 = mybir.dt.int32
+U32 = mybir.dt.uint32
+U16 = mybir.dt.uint16
+U8 = mybir.dt.uint8
+FP8X4 = mybir.dt.float8_e4m3fn_x4
+FP4X4 = mybir.dt.float4_e2m1fn_x4
+ACT = mybir.ActivationFunctionType
+ALU = mybir.AluOpType
+
+P = 128
+PACK = 4
+KP = P * PACK
+PASSES = K // KP
+N = 512
+HALVES = S // N
+MT = S2 // P
+QUADS = 4
+
+
+def tile_list_yarn_substitute_suitability_kernel(
+    tc, tab_words, tab_scales, offs, offs2, w, ws_words, ws_scales, wf_words, wf_scales, gain, out
+):
+    nc = tc.nc
+    with ExitStack() as ctx:
+        keep = ctx.enter_context(tc.tile_pool(name="keep", bufs=1))
+        psum = ctx.enter_context(tc.psum_pool(name="psum", bufs=1))
+
+        def sb(name, shape, dtype):
+            return keep.tile(shape, dtype, name=name, align_bytes=64)
+
+        def bank(i):
+            return psum.tile([P, N], F32, name="bank%d" % i, tag="bank%d" % i)
+
+        list1 = keep.tile([P, S // 16], U16, name="list1")
+        list2 = keep.tile([P, S2 // 16], U16, name="list2")
+        tab_w = [sb("tab_w%d" % a, [P, T], I32) for a in range(PASSES)]
+        tab_s = sb("tab_s", [P, T], U8)
+        wf_w = [sb("wf_w%d" % h, [P, PASSES, N], I32) for h in range(HALVES)]
+        wf_s = sb("wf_s", [P, S], U8)
+        ws_w = sb("ws_w", [P, PASSES, 2 * S2], U8)
+        ws_s = sb("ws_s", [P, PASSES, S2], U8)
+        v_s1 = sb("v_moved", [P, S], U8)
+        w_raw = {(b, a): sb("w_raw%d%d" % (b, a), [P, PACK, KP], F32) for b in range(PASSES) for a in range(PASSES)}
+        gain_t = sb("gain_t", [P, MT], F32)
+        warm = sb("warm", [P, 2], F32)
+
+        nc.vector.memset(tab_s[:].bitcast(I32), 0)
+        nc.vector.memset(wf_s[:].bitcast(I32), 0)
+        nc.vector.memset(ws_s[:].rearrange("p a c -> p (a c)").bitcast(I32), 0)
+        nc.vector.memset(v_s1[:].bitcast(I32), 0)
+
+        def load_w(b, a):
+            nc.sync.dma_start(
+                out=w_raw[b, a][:],
+                in_=w[KP * a : KP * (a + 1), KP * b : KP * (b + 1)].rearrange("(p i) c -> p i c", i=PACK),
+            )
+
+        def load_wf(h):
+            nc.sync.dma_start(
+                out=wf_w[h][:],
+                in_=wf_words[:, :, N * h : N * (h + 1), :].rearrange("a p c i -> p a (c i)").bitcast(I32),
+            )
+
+        nc.sync.dma_start(list2[:], offs2)
+        for q in range(QUADS):
+            nc.scalar.dma_start(
+                out=tab_s[32 * q : 32 * q + 8, :].bitcast(I32), in_=tab_scales[:, 4 * q : 4 * q + 4, :].bitcast(I32)
+            )
+        nc.vector.memset(warm[:, 0:1], 0.0)
+        nc.scalar.activation(warm[:, 1:2], warm[:, 0:1], ACT.Abs)
+        for a in range(PASSES):
+            nc.sync.dma_start(out=tab_w[a][:], in_=tab_words[a].rearrange("p t i -> p (t i)").bitcast(I32))
+        nc.sync.dma_start(list1[:], offs)
+        for q in range(QUADS):
+            nc.sync.dma_start(
+                out=wf_s[32 * q : 32 * q + 8, :].bitcast(I32), in_=wf_scales[:, 4 * q : 4 * q + 4, :].bitcast(I32)
+            )
+        load_wf(0)
+        load_w(0, 0)
+        load_wf(1)
+        for q in range(QUADS):
+            nc.sync.dma_start(
+                out=ws_s[32 * q : 32 * q + 4, :, :].bitcast(I32),
+                in_=ws_scales[:, 4 * q : 4 * q + 4, :].rearrange("a r c -> r a c").bitcast(I32),
+            )
+        nc.sync.dma_start(out=ws_w[:].bitcast(I32), in_=ws_words.rearrange("a p c -> p a c").bitcast(I32))
+        load_w(0, 1)
+        load_w(1, 0)
+        load_w(1, 1)
+        with nc.allow_non_contiguous_dma(reason="one gain value for each partition and row tile"):
+            nc.sync.dma_start(out=gain_t[:], in_=gain.rearrange("(t p) -> p t", p=P))
+
+        v2_w = [sb("v2_w%d" % a, [P, S2], U32) for a in range(PASSES)]
+        v2_s = sb("v2_s", [P, S2], U8)
+        v_w = {(a, h): sb("v_w%d%d" % (a, h), [P, N], U32) for a in range(PASSES) for h in range(HALVES)}
+        v_s = [sb("v_s%d" % h, [P, N], U8) for h in range(HALVES)]
+        nc.vector.tensor_copy(v2_s[:], tab_s[:].indirect(list2[:]))
+        for a in range(PASSES):
+            nc.vector.tensor_copy(v2_w[a][:], tab_w[a][:].bitcast(U32).indirect(list2[:]))
+        for h in range(HALVES):
+            piece = list1[:, (N // 16) * h : (N // 16) * (h + 1)]
+            nc.vector.tensor_copy(v_s[h][:], tab_s[:].indirect(piece))
+            for q in range(QUADS):
+                nc.gpsimd.dma_start(
+                    out=v_s1[32 * q : 32 * q + 4, N * h : N * (h + 1)].bitcast(I32),
+                    in_=v_s[h][32 * q + 4 : 32 * q + 8, :].bitcast(I32),
+                )
+            for a in range(PASSES):
+                nc.vector.tensor_copy(v_w[a, h][:], tab_w[a][:].bitcast(U32).indirect(piece))
+
+        def v2_operand(a, m):
+            cols = slice(P * m, P * (m + 1))
+            return dict(lhsT=v2_w[a][:, cols].bitcast(FP8X4), lhsT_scale=v2_s[4 * a :, cols])
+
+        f_sb = {}
+
+        def stage_f(h):
+            for m in range(MT):
+                acc = bank(m)
+                for a in range(PASSES):
+                    nc.tensor.matmul_mx(
+                        out=acc[:],
+                        rhs=wf_w[h][:, a, :].bitcast(FP8X4),
+                        rhs_scale=wf_s[4 * a :, N * h : N * (h + 1)],
+                        start=(a == 0),
+                        stop=(a == PASSES - 1),
+                        **v2_operand(a, m)
+                    )
+                f_sb[m, h] = sb("f_sb%d%d" % (m, h), [P, N], F32)
+                nc.scalar.copy(f_sb[m, h][:], acc[:])
+
+        w_q = {}
+        w_s = {}
+
+        def quantize_w(b, a, on_scalar):
+            grouped = sb("w_grouped%d%d" % (b, a), [P, KP * PACK], BF16)
+            dst = grouped[:].rearrange("p (t q i) -> p q i t", t=PACK, i=PACK)
+            src = w_raw[b, a][:].rearrange("p i (q t) -> p q i t", t=PACK)
+            if on_scalar:
+                nc.scalar.copy(dst, src)
+            else:
+                nc.vector.tensor_copy(dst, src)
+            w_q[b, a] = sb("w_q%d%d" % (b, a), [P, KP], U32)
+            w_s[b, a] = sb("w_s%d%d" % (b, a), [P, KP], U8)
+            nc.vector.quantize_mx(out=w_q[b, a][:].bitcast(FP8X4), scales=w_s[b, a][:], in_=grouped[:])
+
+        h_q = {}
+        h_s = {}
+
+        def stage_h(b, h, by_pass):
+            accs = [bank(c) for c in range(N // P)]
+            grouped = sb("h_grouped%d%d" % (b, h), [P, N * PACK], BF16)
+
+            def one_pass(c, a):
+                cols = slice(P * c, P * (c + 1))
+                for t in range(PACK):
+                    wc = slice(P * t, P * (t + 1))
+                    nc.tensor.matmul_mx(
+                        out=accs[c][:, wc],
+                        lhsT=w_q[b, a][:, wc].bitcast(FP8X4),
+                        lhsT_scale=w_s[b, a][:, wc],
+                        rhs=v_w[a, h][:, cols].bitcast(FP8X4),
+                        rhs_scale=v_s[h][4 * a :, cols],
+                        start=(a == 0 and t == 0),
+                        stop=(a == PASSES - 1 and t == PACK - 1),
+                    )
+
+            def drain(c):
+                nc.scalar.activation(
+                    grouped[:, N * c : N * (c + 1)].rearrange("p (j t) -> p j t", t=PACK),
+                    accs[c][:].rearrange("p (t j) -> p j t", t=PACK),
+                    ACT.Abs,
+                )
+
+            if by_pass:
+                for c in range(N // P):
+                    one_pass(c, 0)
+                for c in range(N // P):
+                    one_pass(c, 1)
+                    drain(c)
+            else:
+                for c in range(N // P):
+                    one_pass(c, 0)
+                    one_pass(c, 1)
+                    drain(c)
+            h_q[b, h] = sb("h_q%d%d" % (b, h), [P, N], U32)
+            h_s[b, h] = sb("h_s%d%d" % (b, h), [P, N], U8)
+            half = N // 2
+            for u in range(2):
+                nc.vector.quantize_mx(
+                    out=h_q[b, h][:, half * u : half * (u + 1)].bitcast(FP8X4),
+                    scales=h_s[b, h][:, half * u : half * (u + 1)],
+                    in_=grouped[:, PACK * half * u : PACK * half * (u + 1)],
+                )
+
+        e_acc = {}
+
+        def e_skip(m, h, a):
+            if a == 0:
+                e_acc[m, h] = bank(MT * (1 - h) + m)
+            nc.tensor.matmul_mx(
+                out=e_acc[m, h][:],
+                lhsT=ws_w[:, a, 2 * P * m : 2 * P * (m + 1)].bitcast(FP4X4),
+                lhsT_scale=ws_s[:, a, P * m : P * (m + 1)],
+                rhs=v_w[a, h][:].bitcast(FP8X4),
+                rhs_scale=v_s[h][:] if a == 0 else v_s1[:, N * h : N * (h + 1)],
+                start=(a == 0),
+                stop=False,
+            )
+
+        def e_main(m, h, b):
+            nc.tensor.matmul_mx(
+                out=e_acc[m, h][:],
+                rhs=h_q[b, h][:].bitcast(FP8X4),
+                rhs_scale=h_s[b, h][:],
+                start=False,
+                stop=(b == PASSES - 1),
+                **v2_operand(b, m)
+            )
+
+        def finish(m, h):
+            best = sb("best%d%d" % (m, h), [P, N], F32)
+            nc.vector.tensor_tensor(best[:], e_acc[m, h][:], f_sb[m, h][:], ALU.max)
+            res = sb("res%d%d" % (m, h), [P, N], F32)
+            nc.scalar.activation(res[:], best[:], ACT.Copy, scale=gain_t[:, m : m + 1])
+            nc.sync.dma_start(out=out[P * m : P * (m + 1), N * h : N * (h + 1)], in_=res[:])
+
+        stage_f(0)
+        quantize_w(0, 0, True)
+        stage_f(1)
+        quantize_w(0, 1, False)
+        for a in range(PASSES):
+            for m in range(MT):
+                e_skip(m, 0, a)
+        quantize_w(1, 0, False)
+        stage_h(0, 0, True)
+        quantize_w(1, 1, False)
+        stage_h(0, 1, False)
+        for m in range(MT):
+            e_main(m, 0, 0)
+        stage_h(1, 0, False)
+        stage_h(1, 1, False)
+        for m in range(MT):
+            e_main(m, 0, 1)
+            finish(m, 0)
+        for m in range(MT):
+            e_skip(m, 1, 0)
+            e_skip(m, 1, 1)
+            e_main(m, 1, 0)
+            e_main(m, 1, 1)
+            finish(m, 1)

@@ -48,15 +48,15 @@ def tile_list_yarn_substitute_suitability_kernel(
         wf_s = sb("wf_s", [P, S], U8)
         ws_w = sb("ws_w", [P, PASSES, 2 * S2], U8)
         ws_s = sb("ws_s", [P, PASSES, S2], U8)
-        v_s1 = sb("v_moved", [P, S], U8)
+        v_moved = [sb("v_moved%d" % h, [P, N], U8) for h in range(HALVES)]
         w_raw = {(b, a): sb("w_raw%d%d" % (b, a), [P, PACK, KP], F32) for b in range(PASSES) for a in range(PASSES)}
         gain_t = sb("gain_t", [P, MT], F32)
-        warm = sb("warm", [P, 2], F32)
 
         nc.vector.memset(tab_s[:].bitcast(I32), 0)
-        nc.vector.memset(wf_s[:].bitcast(I32), 0)
+        nc.gpsimd.memset(wf_s[:].bitcast(I32), 0)
         nc.vector.memset(ws_s[:].rearrange("p a c -> p (a c)").bitcast(I32), 0)
-        nc.vector.memset(v_s1[:].bitcast(I32), 0)
+        for h in range(HALVES):
+            nc.vector.memset(v_moved[h][:].bitcast(I32), 0)
 
         def load_w(b, a):
             nc.sync.dma_start(
@@ -75,20 +75,18 @@ def tile_list_yarn_substitute_suitability_kernel(
             nc.scalar.dma_start(
                 out=tab_s[32 * q : 32 * q + 8, :].bitcast(I32), in_=tab_scales[:, 4 * q : 4 * q + 4, :].bitcast(I32)
             )
-        nc.vector.memset(warm[:, 0:1], 0.0)
-        nc.scalar.activation(warm[:, 1:2], warm[:, 0:1], ACT.Abs)
         for a in range(PASSES):
             nc.sync.dma_start(out=tab_w[a][:], in_=tab_words[a].rearrange("p t i -> p (t i)").bitcast(I32))
         nc.sync.dma_start(list1[:], offs)
         for q in range(QUADS):
-            nc.sync.dma_start(
+            nc.gpsimd.dma_start(
                 out=wf_s[32 * q : 32 * q + 8, :].bitcast(I32), in_=wf_scales[:, 4 * q : 4 * q + 4, :].bitcast(I32)
             )
         load_wf(0)
         load_w(0, 0)
         load_wf(1)
         for q in range(QUADS):
-            nc.sync.dma_start(
+            nc.gpsimd.dma_start(
                 out=ws_s[32 * q : 32 * q + 4, :, :].bitcast(I32),
                 in_=ws_scales[:, 4 * q : 4 * q + 4, :].rearrange("a r c -> r a c").bitcast(I32),
             )
@@ -111,7 +109,7 @@ def tile_list_yarn_substitute_suitability_kernel(
             nc.vector.tensor_copy(v_s[h][:], tab_s[:].indirect(piece))
             for q in range(QUADS):
                 nc.gpsimd.dma_start(
-                    out=v_s1[32 * q : 32 * q + 4, N * h : N * (h + 1)].bitcast(I32),
+                    out=v_moved[h][32 * q : 32 * q + 4, :].bitcast(I32),
                     in_=v_s[h][32 * q + 4 : 32 * q + 8, :].bitcast(I32),
                 )
             for a in range(PASSES):
@@ -125,7 +123,7 @@ def tile_list_yarn_substitute_suitability_kernel(
 
         def stage_f(h):
             for m in range(MT):
-                acc = bank(m)
+                acc = bank(MT * h + m)
                 for a in range(PASSES):
                     nc.tensor.matmul_mx(
                         out=acc[:],
@@ -136,7 +134,7 @@ def tile_list_yarn_substitute_suitability_kernel(
                         **v2_operand(a, m)
                     )
                 f_sb[m, h] = sb("f_sb%d%d" % (m, h), [P, N], F32)
-                nc.scalar.copy(f_sb[m, h][:], acc[:])
+                nc.scalar.activation(f_sb[m, h][:], acc[:], ACT.Copy)
 
         w_q = {}
         w_s = {}
@@ -202,59 +200,64 @@ def tile_list_yarn_substitute_suitability_kernel(
                     in_=grouped[:, PACK * half * u : PACK * half * (u + 1)],
                 )
 
-        e_acc = {}
+        def e_pass(acc, m, h, cols, step):
+            a = step // 2
+            if step % 2 == 0:
+                width = N if cols.stop - cols.start == N else P
+                for c0 in range(cols.start, cols.stop, width):
+                    part = slice(c0, c0 + width)
+                    nc.tensor.matmul_mx(
+                        out=acc[:, part],
+                        lhsT=ws_w[:, a, 2 * P * m : 2 * P * (m + 1)].bitcast(FP4X4),
+                        lhsT_scale=ws_s[:, a, P * m : P * (m + 1)],
+                        rhs=v_w[a, h][:, part].bitcast(FP8X4),
+                        rhs_scale=(v_s[h] if a == 0 else v_moved[h])[:, part],
+                        start=(step == 0 and c0 == cols.start),
+                        stop=False,
+                    )
+            else:
+                nc.tensor.matmul_mx(
+                    out=acc[:, cols],
+                    rhs=h_q[a, h][:, cols].bitcast(FP8X4),
+                    rhs_scale=h_s[a, h][:, cols],
+                    start=False,
+                    stop=(step == 3),
+                    **v2_operand(a, m)
+                )
 
-        def e_skip(m, h, a):
-            if a == 0:
-                e_acc[m, h] = bank(MT * (1 - h) + m)
-            nc.tensor.matmul_mx(
-                out=e_acc[m, h][:],
-                lhsT=ws_w[:, a, 2 * P * m : 2 * P * (m + 1)].bitcast(FP4X4),
-                lhsT_scale=ws_s[:, a, P * m : P * (m + 1)],
-                rhs=v_w[a, h][:].bitcast(FP8X4),
-                rhs_scale=v_s[h][:] if a == 0 else v_s1[:, N * h : N * (h + 1)],
-                start=(a == 0),
-                stop=False,
-            )
-
-        def e_main(m, h, b):
-            nc.tensor.matmul_mx(
-                out=e_acc[m, h][:],
-                rhs=h_q[b, h][:].bitcast(FP8X4),
-                rhs_scale=h_s[b, h][:],
-                start=False,
-                stop=(b == PASSES - 1),
-                **v2_operand(b, m)
-            )
-
-        def finish(m, h):
-            best = sb("best%d%d" % (m, h), [P, N], F32)
-            nc.vector.tensor_tensor(best[:], e_acc[m, h][:], f_sb[m, h][:], ALU.max)
-            res = sb("res%d%d" % (m, h), [P, N], F32)
+        def finish(acc, m, h, cols):
+            width = cols.stop - cols.start
+            best = sb("best%d%d_%d" % (m, h, cols.start), [P, width], F32)
+            nc.vector.tensor_tensor(best[:], acc[:, cols], f_sb[m, h][:, cols], ALU.max)
+            res = sb("res%d%d_%d" % (m, h, cols.start), [P, width], F32)
             nc.scalar.activation(res[:], best[:], ACT.Copy, scale=gain_t[:, m : m + 1])
-            nc.sync.dma_start(out=out[P * m : P * (m + 1), N * h : N * (h + 1)], in_=res[:])
+            nc.sync.dma_start(
+                out=out[P * m : P * (m + 1), N * h + cols.start : N * h + cols.stop], in_=res[:]
+            )
 
-        stage_f(0)
+        whole = slice(0, N)
         quantize_w(0, 0, True)
+        stage_f(0)
         stage_f(1)
         quantize_w(0, 1, False)
-        for a in range(PASSES):
-            for m in range(MT):
-                e_skip(m, 0, a)
+        first = [bank(MT + m) for m in range(MT)]
+        for m in range(MT):
+            e_pass(first[m], m, 0, whole, 0)
         quantize_w(1, 0, False)
         stage_h(0, 0, True)
         quantize_w(1, 1, False)
         stage_h(0, 1, False)
-        for m in range(MT):
-            e_main(m, 0, 0)
+        for step in (1, 2):
+            for m in range(MT):
+                e_pass(first[m], m, 0, whole, step)
         stage_h(1, 0, False)
         stage_h(1, 1, False)
         for m in range(MT):
-            e_main(m, 0, 1)
-            finish(m, 0)
-        for m in range(MT):
-            e_skip(m, 1, 0)
-            e_skip(m, 1, 1)
-            e_main(m, 1, 0)
-            e_main(m, 1, 1)
-            finish(m, 1)
+            e_pass(first[m], m, 0, whole, 3)
+            finish(first[m], m, 0, whole)
+        pieces = [(m, whole) for m in range(MT - 1)] + [(MT - 1, slice(0, N // 2)), (MT - 1, slice(N // 2, N))]
+        for i, (m, cols) in enumerate(pieces):
+            acc = bank(i)
+            for step in range(4):
+                e_pass(acc, m, 1, cols, step)
+            finish(acc, m, 1, cols)

@@ -44,76 +44,92 @@ def tile_list_yarn_substitute_suitability_kernel(
         list2 = keep.tile([P, S2 // 16], U16, name="list2")
         tab_w = [sb("tab_w%d" % a, [P, T], I32) for a in range(PASSES)]
         tab_s = sb("tab_s", [P, T], U8)
-        wf_w = [sb("wf_w%d" % h, [P, PASSES, N], I32) for h in range(HALVES)]
-        wf_s = sb("wf_s", [P, S], U8)
+        wf_w = [sb("wf_w%d" % a, [P, S], I32) for a in range(PASSES)]
+        wf_s = sb("wf_s", [P, PASSES, S], U8)
         ws_w = sb("ws_w", [P, PASSES, 2 * S2], U8)
         ws_s = sb("ws_s", [P, PASSES, S2], U8)
-        v_moved = [sb("v_moved%d" % h, [P, N], U8) for h in range(HALVES)]
-        w_raw = {(b, a): sb("w_raw%d%d" % (b, a), [P, PACK, KP], F32) for b in range(PASSES) for a in range(PASSES)}
+        v_moved = sb("v_moved", [P, S], U8)
+        w_raw = {}
         gain_t = sb("gain_t", [P, MT], F32)
 
         nc.vector.memset(tab_s[:].bitcast(I32), 0)
-        nc.gpsimd.memset(wf_s[:].bitcast(I32), 0)
+        nc.vector.memset(wf_s[:].rearrange("p a c -> p (a c)").bitcast(I32), 0)
         nc.vector.memset(ws_s[:].rearrange("p a c -> p (a c)").bitcast(I32), 0)
-        for h in range(HALVES):
-            nc.vector.memset(v_moved[h][:].bitcast(I32), 0)
+        nc.vector.memset(v_moved[:].bitcast(I32), 0)
 
-        def load_w(b, a):
-            nc.sync.dma_start(
-                out=w_raw[b, a][:],
-                in_=w[KP * a : KP * (a + 1), KP * b : KP * (b + 1)].rearrange("(p i) c -> p i c", i=PACK),
-            )
+        def load_w(b, a, pieces):
+            width = KP // pieces
+            w_raw[b, a] = []
+            for u in range(pieces):
+                raw = sb("w_raw%d%d%d" % (b, a, u), [P, PACK, width], F32)
+                c0 = KP * b + width * u
+                nc.sync.dma_start(
+                    out=raw[:], in_=w[KP * a : KP * (a + 1), c0 : c0 + width].rearrange("(p i) c -> p i c", i=PACK)
+                )
+                w_raw[b, a].append(raw)
 
-        def load_wf(h):
-            nc.sync.dma_start(
-                out=wf_w[h][:],
-                in_=wf_words[:, :, N * h : N * (h + 1), :].rearrange("a p c i -> p a (c i)").bitcast(I32),
-            )
+        def load_wf(a):
+            nc.sync.dma_start(out=wf_w[a][:], in_=wf_words[a].rearrange("p c i -> p (c i)").bitcast(I32))
 
         nc.sync.dma_start(list2[:], offs2)
-        for q in range(QUADS):
-            nc.scalar.dma_start(
-                out=tab_s[32 * q : 32 * q + 8, :].bitcast(I32), in_=tab_scales[:, 4 * q : 4 * q + 4, :].bitcast(I32)
-            )
-        for a in range(PASSES):
-            nc.sync.dma_start(out=tab_w[a][:], in_=tab_words[a].rearrange("p t i -> p (t i)").bitcast(I32))
         nc.sync.dma_start(list1[:], offs)
         for q in range(QUADS):
-            nc.gpsimd.dma_start(
-                out=wf_s[32 * q : 32 * q + 8, :].bitcast(I32), in_=wf_scales[:, 4 * q : 4 * q + 4, :].bitcast(I32)
+            (nc.sync if q < QUADS // 2 else nc.scalar).dma_start(
+                out=tab_s[32 * q : 32 * q + 8, :].bitcast(I32), in_=tab_scales[:, 4 * q : 4 * q + 4, :].bitcast(I32)
             )
+        def load_tab(a):
+            nc.sync.dma_start(out=tab_w[a][:], in_=tab_words[a].rearrange("p t i -> p (t i)").bitcast(I32))
+
+        load_tab(0)
         load_wf(0)
-        load_w(0, 0)
-        load_wf(1)
         for q in range(QUADS):
-            nc.gpsimd.dma_start(
+            nc.sync.dma_start(
+                out=wf_s[32 * q : 32 * q + 4, :, :].bitcast(I32),
+                in_=wf_scales[:, 4 * q : 4 * q + 4, :].rearrange("a r c -> r a c").bitcast(I32),
+            )
+        load_tab(1)
+        load_wf(1)
+        load_w(0, 0, 2)
+        for q in range(QUADS):
+            nc.sync.dma_start(
                 out=ws_s[32 * q : 32 * q + 4, :, :].bitcast(I32),
                 in_=ws_scales[:, 4 * q : 4 * q + 4, :].rearrange("a r c -> r a c").bitcast(I32),
             )
         nc.sync.dma_start(out=ws_w[:].bitcast(I32), in_=ws_words.rearrange("a p c -> p a c").bitcast(I32))
-        load_w(0, 1)
-        load_w(1, 0)
-        load_w(1, 1)
-        with nc.allow_non_contiguous_dma(reason="one gain value for each partition and row tile"):
-            nc.sync.dma_start(out=gain_t[:], in_=gain.rearrange("(t p) -> p t", p=P))
+        load_w(0, 1, 2)
 
         v2_w = [sb("v2_w%d" % a, [P, S2], U32) for a in range(PASSES)]
         v2_s = sb("v2_s", [P, S2], U8)
-        v_w = {(a, h): sb("v_w%d%d" % (a, h), [P, N], U32) for a in range(PASSES) for h in range(HALVES)}
-        v_s = [sb("v_s%d" % h, [P, N], U8) for h in range(HALVES)]
+        v_w = {}
+        v_s = {}
+
+        def piece(h):
+            return list1[:, (N // 16) * h : (N // 16) * (h + 1)]
+
+        def gather_scales(h, tag):
+            v_s[h] = keep.tile([P, N], U8, name="v_s%d" % h, tag=tag, align_bytes=64)
+            nc.vector.tensor_copy(v_s[h][:], tab_s[:].indirect(piece(h)))
+            for q in range(QUADS):
+                nc.sync.dma_start(
+                    out=v_moved[32 * q : 32 * q + 4, N * h : N * (h + 1)].bitcast(I32),
+                    in_=v_s[h][32 * q + 4 : 32 * q + 8, :].bitcast(I32),
+                )
+
+        def gather_words(h, tag):
+            both = keep.tile([P, PASSES * N], U32, name="v_w%d" % h, tag=tag, align_bytes=64)
+            for a in range(PASSES):
+                v_w[a, h] = both[:, N * a : N * (a + 1)]
+                nc.vector.tensor_copy(v_w[a, h], tab_w[a][:].bitcast(U32).indirect(piece(h)))
+
         nc.vector.tensor_copy(v2_s[:], tab_s[:].indirect(list2[:]))
         for a in range(PASSES):
             nc.vector.tensor_copy(v2_w[a][:], tab_w[a][:].bitcast(U32).indirect(list2[:]))
-        for h in range(HALVES):
-            piece = list1[:, (N // 16) * h : (N // 16) * (h + 1)]
-            nc.vector.tensor_copy(v_s[h][:], tab_s[:].indirect(piece))
-            for q in range(QUADS):
-                nc.gpsimd.dma_start(
-                    out=v_moved[h][32 * q : 32 * q + 4, :].bitcast(I32),
-                    in_=v_s[h][32 * q + 4 : 32 * q + 8, :].bitcast(I32),
-                )
-            for a in range(PASSES):
-                nc.vector.tensor_copy(v_w[a, h][:], tab_w[a][:].bitcast(U32).indirect(piece))
+        gather_scales(0, "v_s0")
+        gather_words(0, "v_w0")
+        load_w(1, 0, 1)
+        load_w(1, 1, 1)
+        with nc.allow_non_contiguous_dma(reason="one gain value for each partition and row tile"):
+            nc.sync.dma_start(out=gain_t[:], in_=gain.rearrange("(t p) -> p t", p=P))
 
         def v2_operand(a, m):
             cols = slice(P * m, P * (m + 1))
@@ -121,20 +137,21 @@ def tile_list_yarn_substitute_suitability_kernel(
 
         f_sb = {}
 
-        def stage_f(h):
-            for m in range(MT):
-                acc = bank(MT * h + m)
-                for a in range(PASSES):
+        def stage_f():
+            accs = {(m, h): bank(MT * h + m) for h in range(HALVES) for m in range(MT)}
+            for a in range(PASSES):
+                for (m, h), acc in accs.items():
                     nc.tensor.matmul_mx(
                         out=acc[:],
-                        rhs=wf_w[h][:, a, :].bitcast(FP8X4),
-                        rhs_scale=wf_s[4 * a :, N * h : N * (h + 1)],
+                        rhs=wf_w[a][:, N * h : N * (h + 1)].bitcast(FP8X4),
+                        rhs_scale=wf_s[:, a, N * h : N * (h + 1)],
                         start=(a == 0),
                         stop=(a == PASSES - 1),
                         **v2_operand(a, m)
                     )
-                f_sb[m, h] = sb("f_sb%d%d" % (m, h), [P, N], F32)
-                nc.scalar.activation(f_sb[m, h][:], acc[:], ACT.Copy)
+                    if a == PASSES - 1:
+                        f_sb[m, h] = sb("f_sb%d%d" % (m, h), [P, N], F32)
+                        nc.scalar.activation(f_sb[m, h][:], acc[:], ACT.Copy)
 
         w_q = {}
         w_s = {}
@@ -142,11 +159,14 @@ def tile_list_yarn_substitute_suitability_kernel(
         def quantize_w(b, a, on_scalar):
             grouped = sb("w_grouped%d%d" % (b, a), [P, KP * PACK], BF16)
             dst = grouped[:].rearrange("p (t q i) -> p q i t", t=PACK, i=PACK)
-            src = w_raw[b, a][:].rearrange("p i (q t) -> p q i t", t=PACK)
-            if on_scalar:
-                nc.scalar.copy(dst, src)
-            else:
-                nc.vector.tensor_copy(dst, src)
+            share = P // len(w_raw[b, a])
+            for u, raw in enumerate(w_raw[b, a]):
+                src = raw[:].rearrange("p i (q t) -> p q i t", t=PACK)
+                part = dst[:, share * u : share * (u + 1), :, :]
+                if on_scalar:
+                    nc.scalar.copy(part, src)
+                else:
+                    nc.vector.tensor_copy(part, src)
             w_q[b, a] = sb("w_q%d%d" % (b, a), [P, KP], U32)
             w_s[b, a] = sb("w_s%d%d" % (b, a), [P, KP], U8)
             nc.vector.quantize_mx(out=w_q[b, a][:].bitcast(FP8X4), scales=w_s[b, a][:], in_=grouped[:])
@@ -190,7 +210,11 @@ def tile_list_yarn_substitute_suitability_kernel(
                     one_pass(c, 0)
                     one_pass(c, 1)
                     drain(c)
-            h_q[b, h] = sb("h_q%d%d" % (b, h), [P, N], U32)
+            if h == 0:
+                tag = "w_grouped11" if b == 0 else "h_q%d" % b
+                both = keep.tile([P, S], U32, name="h_q%d" % b, tag=tag, align_bytes=64)
+                for u in range(HALVES):
+                    h_q[b, u] = both[:, N * u : N * (u + 1)]
             h_s[b, h] = sb("h_s%d%d" % (b, h), [P, N], U8)
             half = N // 2
             for u in range(2):
@@ -201,8 +225,8 @@ def tile_list_yarn_substitute_suitability_kernel(
                 )
 
         def e_pass(acc, m, h, cols, step):
-            a = step // 2
-            if step % 2 == 0:
+            a = step % 2
+            if step < 2:
                 width = N if cols.stop - cols.start == N else P
                 for c0 in range(cols.start, cols.stop, width):
                     part = slice(c0, c0 + width)
@@ -211,7 +235,7 @@ def tile_list_yarn_substitute_suitability_kernel(
                         lhsT=ws_w[:, a, 2 * P * m : 2 * P * (m + 1)].bitcast(FP4X4),
                         lhsT_scale=ws_s[:, a, P * m : P * (m + 1)],
                         rhs=v_w[a, h][:, part].bitcast(FP8X4),
-                        rhs_scale=(v_s[h] if a == 0 else v_moved[h])[:, part],
+                        rhs_scale=v_s[h][:, part] if a == 0 else v_moved[:, N * h + c0 : N * h + c0 + width],
                         start=(step == 0 and c0 == cols.start),
                         stop=False,
                     )
@@ -230,32 +254,37 @@ def tile_list_yarn_substitute_suitability_kernel(
             best = sb("best%d%d_%d" % (m, h, cols.start), [P, width], F32)
             nc.vector.tensor_tensor(best[:], acc[:, cols], f_sb[m, h][:, cols], ALU.max)
             res = sb("res%d%d_%d" % (m, h, cols.start), [P, width], F32)
-            nc.scalar.activation(res[:], best[:], ACT.Copy, scale=gain_t[:, m : m + 1])
+            if (m, h, cols) == (MT - 1, HALVES - 1, slice(N - P, N)):
+                nc.vector.tensor_scalar(res[:], best[:], gain_t[:, m : m + 1], None, ALU.mult)
+            else:
+                nc.scalar.activation(res[:], best[:], ACT.Copy, scale=gain_t[:, m : m + 1])
             nc.sync.dma_start(
                 out=out[P * m : P * (m + 1), N * h + cols.start : N * h + cols.stop], in_=res[:]
             )
 
         whole = slice(0, N)
-        quantize_w(0, 0, True)
-        stage_f(0)
-        stage_f(1)
+        quantize_w(0, 0, False)
+        gather_scales(1, "w_raw000")
+        stage_f()
         quantize_w(0, 1, False)
-        first = [bank(MT + m) for m in range(MT)]
-        for m in range(MT):
-            e_pass(first[m], m, 0, whole, 0)
+        gather_words(1, "w_grouped01")
         quantize_w(1, 0, False)
-        stage_h(0, 0, True)
-        quantize_w(1, 1, False)
-        stage_h(0, 1, False)
-        for step in (1, 2):
+        first = [bank(MT + m) for m in range(MT)]
+        for step in (0, 1):
             for m in range(MT):
                 e_pass(first[m], m, 0, whole, step)
-        stage_h(1, 0, False)
+        quantize_w(1, 1, False)
+        stage_h(0, 0, True)
+        stage_h(0, 1, False)
+        stage_h(1, 0, True)
+        for m in range(MT):
+            e_pass(first[m], m, 0, whole, 2)
         stage_h(1, 1, False)
         for m in range(MT):
             e_pass(first[m], m, 0, whole, 3)
             finish(first[m], m, 0, whole)
-        pieces = [(m, whole) for m in range(MT - 1)] + [(MT - 1, slice(0, N // 2)), (MT - 1, slice(N // 2, N))]
+        last = [slice(0, N // 2), slice(N // 2, N - P), slice(N - P, N)]
+        pieces = [(m, whole) for m in range(MT - 1)] + [(MT - 1, cols) for cols in last]
         for i, (m, cols) in enumerate(pieces):
             acc = bank(i)
             for step in range(4):

from contextlib import ExitStack

import concourse.mybir as mybir

K, T, S, S2 = 1024, 2048, 1024, 512
FLOPS = 2 * K * K * S + 3 * 2 * K * S2 * S

F32 = mybir.dt.float32
BF16 = mybir.dt.bfloat16
I32 = mybir.dt.int32
U32 = mybir.dt.uint32
U16 = mybir.dt.uint16
U8 = mybir.dt.uint8
FP8X4 = mybir.dt.float8_e4m3fn_x4
FP4X4 = mybir.dt.float4_e2m1fn_x4
ACT = mybir.ActivationFunctionType
ALU = mybir.AluOpType

P = 128
PACK = 4
KP = P * PACK
PASSES = K // KP
N = 512
HALVES = S // N
MT = S2 // P
QUADS = 4


def tile_list_yarn_substitute_suitability_kernel(
    tc, tab_words, tab_scales, offs, offs2, w, ws_words, ws_scales, wf_words, wf_scales, gain, out
):
    nc = tc.nc
    with ExitStack() as ctx:
        keep = ctx.enter_context(tc.tile_pool(name="keep", bufs=1))
        psum = ctx.enter_context(tc.psum_pool(name="psum", bufs=1))

        def sb(name, shape, dtype):
            return keep.tile(shape, dtype, name=name, align_bytes=64)

        def bank(i):
            return psum.tile([P, N], F32, name="bank%d" % i, tag="bank%d" % i)

        list1 = keep.tile([P, S // 16], U16, name="list1")
        list2 = keep.tile([P, S2 // 16], U16, name="list2")
        tab_w = [sb("tab_w%d" % a, [P, T], I32) for a in range(PASSES)]
        tab_s = sb("tab_s", [P, T], U8)
        wf_w = [sb("wf_w%d" % a, [P, S], I32) for a in range(PASSES)]
        wf_s = sb("wf_s", [P, PASSES, S], U8)
        ws_w = sb("ws_w", [P, PASSES, 2 * S2], U8)
        ws_s = sb("ws_s", [P, PASSES, S2], U8)
        v_moved = sb("v_moved", [P, S], U8)
        w_raw = {}
        gain_t = sb("gain_t", [P, MT], F32)

        nc.vector.memset(tab_s[:].bitcast(I32), 0)
        nc.vector.memset(wf_s[:].rearrange("p a c -> p (a c)").bitcast(I32), 0)
        nc.vector.memset(ws_s[:].rearrange("p a c -> p (a c)").bitcast(I32), 0)
        nc.vector.memset(v_moved[:].bitcast(I32), 0)

        def load_w(b, a, pieces):
            width = KP // pieces
            w_raw[b, a] = []
            for u in range(pieces):
                raw = sb("w_raw%d%d%d" % (b, a, u), [P, PACK, width], F32)
                c0 = KP * b + width * u
                nc.sync.dma_start(
                    out=raw[:], in_=w[KP * a : KP * (a + 1), c0 : c0 + width].rearrange("(p i) c -> p i c", i=PACK)
                )
                w_raw[b, a].append(raw)

        def load_wf(a):
            nc.sync.dma_start(out=wf_w[a][:], in_=wf_words[a].rearrange("p c i -> p (c i)").bitcast(I32))

        nc.sync.dma_start(list2[:], offs2)
        nc.sync.dma_start(list1[:], offs)
        for q in range(QUADS):
            (nc.sync if q < QUADS // 2 else nc.scalar).dma_start(
                out=tab_s[32 * q : 32 * q + 8, :].bitcast(I32), in_=tab_scales[:, 4 * q : 4 * q + 4, :].bitcast(I32)
            )
        def load_tab(a):
            nc.sync.dma_start(out=tab_w[a][:], in_=tab_words[a].rearrange("p t i -> p (t i)").bitcast(I32))

        load_tab(0)
        load_wf(0)
        for q in range(QUADS):
            nc.sync.dma_start(
                out=wf_s[32 * q : 32 * q + 4, :, :].bitcast(I32),
                in_=wf_scales[:, 4 * q : 4 * q + 4, :].rearrange("a r c -> r a c").bitcast(I32),
            )
        load_tab(1)
        load_wf(1)
        load_w(0, 0, 2)
        for q in range(QUADS):
            nc.sync.dma_start(
                out=ws_s[32 * q : 32 * q + 4, :, :].bitcast(I32),
                in_=ws_scales[:, 4 * q : 4 * q + 4, :].rearrange("a r c -> r a c").bitcast(I32),
            )
        nc.sync.dma_start(out=ws_w[:].bitcast(I32), in_=ws_words.rearrange("a p c -> p a c").bitcast(I32))
        load_w(0, 1, 2)

        v2_w = [sb("v2_w%d" % a, [P, S2], U32) for a in range(PASSES)]
        v2_s = sb("v2_s", [P, S2], U8)
        v_w = {}
        v_s = {}

        def piece(h):
            return list1[:, (N // 16) * h : (N // 16) * (h + 1)]

        def gather_scales(h, tag):
            v_s[h] = keep.tile([P, N], U8, name="v_s%d" % h, tag=tag, align_bytes=64)
            nc.vector.tensor_copy(v_s[h][:], tab_s[:].indirect(piece(h)))
            for q in range(QUADS):
                nc.sync.dma_start(
                    out=v_moved[32 * q : 32 * q + 4, N * h : N * (h + 1)].bitcast(I32),
                    in_=v_s[h][32 * q + 4 : 32 * q + 8, :].bitcast(I32),
                )

        def gather_words(h, tag):
            both = keep.tile([P, PASSES * N], U32, name="v_w%d" % h, tag=tag, align_bytes=64)
            for a in range(PASSES):
                v_w[a, h] = both[:, N * a : N * (a + 1)]
                nc.vector.tensor_copy(v_w[a, h], tab_w[a][:].bitcast(U32).indirect(piece(h)))

        nc.vector.tensor_copy(v2_s[:], tab_s[:].indirect(list2[:]))
        for a in range(PASSES):
            nc.vector.tensor_copy(v2_w[a][:], tab_w[a][:].bitcast(U32).indirect(list2[:]))
        gather_scales(0, "v_s0")
        gather_words(0, "v_w0")
        load_w(1, 0, 1)
        load_w(1, 1, 1)
        with nc.allow_non_contiguous_dma(reason="one gain value for each partition and row tile"):
            nc.sync.dma_start(out=gain_t[:], in_=gain.rearrange("(t p) -> p t", p=P))

        def v2_operand(a, m):
            cols = slice(P * m, P * (m + 1))
            return dict(lhsT=v2_w[a][:, cols].bitcast(FP8X4), lhsT_scale=v2_s[4 * a :, cols])

        f_sb = {}

        def stage_f():
            accs = {(m, h): bank(MT * h + m) for h in range(HALVES) for m in range(MT)}
            for a in range(PASSES):
                for (m, h), acc in accs.items():
                    nc.tensor.matmul_mx(
                        out=acc[:],
                        rhs=wf_w[a][:, N * h : N * (h + 1)].bitcast(FP8X4),
                        rhs_scale=wf_s[:, a, N * h : N * (h + 1)],
                        start=(a == 0),
                        stop=(a == PASSES - 1),
                        **v2_operand(a, m)
                    )
                    if a == PASSES - 1:
                        f_sb[m, h] = sb("f_sb%d%d" % (m, h), [P, N], F32)
                        nc.scalar.activation(f_sb[m, h][:], acc[:], ACT.Copy)

        w_q = {}
        w_s = {}

        def quantize_w(b, a, on_scalar):
            grouped = sb("w_grouped%d%d" % (b, a), [P, KP * PACK], BF16)
            dst = grouped[:].rearrange("p (t q i) -> p q i t", t=PACK, i=PACK)
            share = P // len(w_raw[b, a])
            for u, raw in enumerate(w_raw[b, a]):
                src = raw[:].rearrange("p i (q t) -> p q i t", t=PACK)
                part = dst[:, share * u : share * (u + 1), :, :]
                if on_scalar:
                    nc.scalar.copy(part, src)
                else:
                    nc.vector.tensor_copy(part, src)
            w_q[b, a] = sb("w_q%d%d" % (b, a), [P, KP], U32)
            w_s[b, a] = sb("w_s%d%d" % (b, a), [P, KP], U8)
            nc.vector.quantize_mx(out=w_q[b, a][:].bitcast(FP8X4), scales=w_s[b, a][:], in_=grouped[:])

        h_q = {}
        h_s = {}

        def stage_h(b, h, by_pass):
            accs = [bank(c) for c in range(N // P)]
            grouped = sb("h_grouped%d%d" % (b, h), [P, N * PACK], BF16)

            def one_pass(c, a):
                cols = slice(P * c, P * (c + 1))
                for t in range(PACK):
                    wc = slice(P * t, P * (t + 1))
                    nc.tensor.matmul_mx(
                        out=accs[c][:, wc],
                        lhsT=w_q[b, a][:, wc].bitcast(FP8X4),
                        lhsT_scale=w_s[b, a][:, wc],
                        rhs=v_w[a, h][:, cols].bitcast(FP8X4),
                        rhs_scale=v_s[h][4 * a :, cols],
                        start=(a == 0 and t == 0),
                        stop=(a == PASSES - 1 and t == PACK - 1),
                    )

            def drain(c):
                nc.scalar.activation(
                    grouped[:, N * c : N * (c + 1)].rearrange("p (j t) -> p j t", t=PACK),
                    accs[c][:].rearrange("p (t j) -> p j t", t=PACK),
                    ACT.Abs,
                )

            if by_pass:
                for c in range(N // P):
                    one_pass(c, 0)
                for c in range(N // P):
                    one_pass(c, 1)
                    drain(c)
            else:
                for c in range(N // P):
                    one_pass(c, 0)
                    one_pass(c, 1)
                    drain(c)
            if h == 0:
                tag = "w_grouped11" if b == 0 else "h_q%d" % b
                both = keep.tile([P, S], U32, name="h_q%d" % b, tag=tag, align_bytes=64)
                for u in range(HALVES):
                    h_q[b, u] = both[:, N * u : N * (u + 1)]
            h_s[b, h] = sb("h_s%d%d" % (b, h), [P, N], U8)
            half = N // 2
            for u in range(2):
                nc.vector.quantize_mx(
                    out=h_q[b, h][:, half * u : half * (u + 1)].bitcast(FP8X4),
                    scales=h_s[b, h][:, half * u : half * (u + 1)],
                    in_=grouped[:, PACK * half * u : PACK * half * (u + 1)],
                )

        def e_pass(acc, m, h, cols, step):
            a = step % 2
            if step < 2:
                width = N if cols.stop - cols.start == N else P
                for c0 in range(cols.start, cols.stop, width):
                    part = slice(c0, c0 + width)
                    nc.tensor.matmul_mx(
                        out=acc[:, part],
                        lhsT=ws_w[:, a, 2 * P * m : 2 * P * (m + 1)].bitcast(FP4X4),
                        lhsT_scale=ws_s[:, a, P * m : P * (m + 1)],
                        rhs=v_w[a, h][:, part].bitcast(FP8X4),
                        rhs_scale=v_s[h][:, part] if a == 0 else v_moved[:, N * h + c0 : N * h + c0 + width],
                        start=(step == 0 and c0 == cols.start),
                        stop=False,
                    )
            else:
                nc.tensor.matmul_mx(
                    out=acc[:, cols],
                    rhs=h_q[a, h][:, cols].bitcast(FP8X4),
                    rhs_scale=h_s[a, h][:, cols],
                    start=False,
                    stop=(step == 3),
                    **v2_operand(a, m)
                )

        def finish(acc, m, h, cols):
            width = cols.stop - cols.start
            best = sb("best%d%d_%d" % (m, h, cols.start), [P, width], F32)
            nc.vector.tensor_tensor(best[:], acc[:, cols], f_sb[m, h][:, cols], ALU.max)
            res = sb("res%d%d_%d" % (m, h, cols.start), [P, width], F32)
            if (m, h, cols) == (MT - 1, HALVES - 1, slice(N - P, N)):
                nc.vector.tensor_scalar(res[:], best[:], gain_t[:, m : m + 1], None, ALU.mult)
            else:
                nc.scalar.activation(res[:], best[:], ACT.Copy, scale=gain_t[:, m : m + 1])
            nc.sync.dma_start(
                out=out[P * m : P * (m + 1), N * h + cols.start : N * h + cols.stop], in_=res[:]
            )

        whole = slice(0, N)
        quantize_w(0, 0, False)
        gather_scales(1, "w_raw000")
        stage_f()
        quantize_w(0, 1, False)
        gather_words(1, "w_grouped01")
        quantize_w(1, 0, False)
        first = [bank(MT + m) for m in range(MT)]
        for step in (0, 1):
            for m in range(MT):
                e_pass(first[m], m, 0, whole, step)
        quantize_w(1, 1, False)
        stage_h(0, 0, True)
        stage_h(0, 1, False)
        stage_h(1, 0, True)
        for m in range(MT):
            e_pass(first[m], m, 0, whole, 2)
        stage_h(1, 1, False)
        for m in range(MT):
            e_pass(first[m], m, 0, whole, 3)
            finish(first[m], m, 0, whole)
        last = [slice(0, N // 2), slice(N // 2, N - P), slice(N - P, N)]
        pieces = [(m, whole) for m in range(MT - 1)] + [(MT - 1, cols) for cols in last]
        for i, (m, cols) in enumerate(pieces):
            acc = bank(i)
            for step in range(4):
                e_pass(acc, m, 1, cols, step)
            finish(acc, m, 1, cols)
